import numpy as np
import ml_dtypes


def mxq(x, axis, fmt="e4m3"):
    dtype, down = {"e4m3": (ml_dtypes.float8_e4m3fn, 7), "e5m2": (ml_dtypes.float8_e5m2, 14)}[fmt]
    v = np.moveaxis(np.asarray(x, np.float32).astype(ml_dtypes.bfloat16).astype(np.float64), axis, -1)
    blocks = v.reshape(v.shape[:-1] + (-1, 32))
    amax = np.abs(blocks).max(-1, keepdims=True)
    byte = np.maximum(np.where(amax > 0, np.frexp(amax)[1] - 1 + 127, 0) - down, 1)
    scale = np.exp2(byte - 127.0)
    codes = (blocks / scale).astype(np.float32).astype(dtype).astype(np.float64)
    return np.moveaxis((codes * scale).reshape(v.shape), -1, axis)


WIDE = False


def mx_kscale(k):
    if not WIDE:
        return np.ones(k)
    levels = np.array([10, -10, 5, -5, 0])
    if k % 512:
        return np.exp2(np.random.permutation(np.resize(levels, k // 32))).repeat(32)
    a = np.empty((k // 512, 16))
    for p in range(k // 512):
        a[p, :8] = np.random.permutation(np.resize(levels, 8))
        for g in range(8):
            far = levels[np.abs(levels - a[p, g]) >= 10]
            a[p, g + 8] = far[np.random.randint(len(far))]
    return np.exp2(a.ravel()).repeat(32)


def f64(x):
    return np.asarray(x).astype(np.float64)


def striped(idx):
    return np.tile(np.asarray(idx).reshape(-1, 16).T, (8, 1)).astype(np.uint16)


def unstriped(offs):
    return offs[:16].T.reshape(-1).astype(np.int64)


def striped8(idx):
    return np.asarray(idx).reshape(8, -1, 16).transpose(0, 2, 1).reshape(128, -1).astype(np.uint16)


def unstriped8(offs):
    return offs.reshape(8, 16, -1).transpose(0, 2, 1).reshape(8, -1).astype(np.int64)


def pick8(x, idx, run):
    r = np.arange(len(x))
    return x[r[:, None], idx[r % (8 * run) // run]]


E2M1 = np.array([0.0, 0.5, 1.0, 1.5, 2.0, 3.0, 4.0, 6.0, -0.0, -0.5, -1.0, -1.5, -2.0, -3.0, -4.0, -6.0])


def pack_weight(w, fmt):
    k, n = w.shape
    w = f64(np.asarray(w, np.float32).astype(ml_dtypes.bfloat16)).reshape(k // 32, 32, n)
    amax = np.abs(w).max(1)
    if fmt == "e4m3":
        byte = np.frexp(amax)[1] - 1 + 127 - 7
    else:
        mant, ex = np.frexp(amax / 6.0)
        byte = np.where(mant > 0.5, ex, ex - 1) + 127
    byte = np.clip(np.where(amax > 0, byte, 1), 1, 254)
    scaled = (w * np.exp2(127.0 - byte)[:, None, :]).reshape(k, n).astype(np.float32)
    by_word = np.ascontiguousarray(scaled.reshape(k // 512, 128, 4, n).transpose(0, 1, 3, 2))
    if fmt == "e4m3":
        words = by_word.astype(ml_dtypes.float8_e4m3fn).view(np.uint8)
    else:
        c = by_word.astype(ml_dtypes.float4_e2m1fn).view(np.uint8) & 0xF
        words = (c[..., 0::2] | (c[..., 1::2] << 4)).reshape(k // 512, 128, 2 * n)
    return np.ascontiguousarray(words), np.ascontiguousarray(byte.astype(np.uint8).reshape(k // 512, 16, n))


def unpack_weight(words, scales, fmt):
    g, _, n = scales.shape
    words = np.ascontiguousarray(words).reshape(g, 128, n, -1)
    if fmt == "e4m3":
        vals = words.view(ml_dtypes.float8_e4m3fn).astype(np.float64)
    else:
        nib = np.empty((g, 128, n, 4), np.uint8)
        nib[..., 0::2] = words & 0xF
        nib[..., 1::2] = words >> 4
        vals = E2M1[nib]
    vals = vals * np.repeat(np.exp2(scales.astype(np.float64) - 127.0), 8, axis=1)[..., None]
    return vals.transpose(0, 1, 3, 2).reshape(g * 512, n)


K, J, R, T, C, D, O, S, N, Z = 512, 256, 512, 1024, 512, 512, 256, 128, 256, 1024


def setup_inputs():
    n = np.random.standard_normal
    idx = np.random.permutation(T)[:J]
    idx2 = np.stack([np.random.permutation(C)[:J] for _ in range(8)])
    idx3 = np.stack([np.random.permutation(C)[:S] for _ in range(8)])
    idx4 = np.stack([np.random.permutation(D)[:S] for _ in range(8)])
    idx5 = np.stack([np.random.permutation(D)[:J] for _ in range(8)])
    idx6 = np.stack([np.random.permutation(D)[:O] for _ in range(8)])
    idx7 = np.random.permutation(Z)[:N]
    fk = mx_kscale(K)
    fr = mx_kscale(R)
    xtp = pack_weight(n((K, T)) * fk[:, None], "e4m3")
    wp = pack_weight(n((K, R)) * 1 / np.sqrt(K) / fk[:, None] * fr, "e4m3")
    w2p = pack_weight(n((K, R)) * 1 / np.sqrt(K) / fk[:, None] * fr, "e2m1")
    vsp = pack_weight(n((R, Z)) * 1 / np.sqrt(R) / fr[:, None], "e2m1")
    return {
        "xt_words": xtp[0],
        "xt_scales": xtp[1],
        "w_words": wp[0],
        "w_scales": wp[1],
        "w2_words": w2p[0],
        "w2_scales": w2p[1],
        "sa": (np.random.uniform(0.5, 1.6, (R, 1))).astype(np.float32),
        "sb": (np.random.uniform(0.5, 1.6, (R, 1))).astype(np.float32),
        "vs_words": vsp[0],
        "vs_scales": vsp[1],
        "offs": striped(idx),
        "offs2": striped8(idx2),
        "offs3": striped8(idx3),
        "offs4": striped8(idx4),
        "offs5": striped8(idx5),
        "offs6": striped8(idx6),
        "offs7": striped(idx7),
    }


def reference(xt_words, xt_scales, w_words, w_scales, w2_words, w2_scales, sa, sb, vs_words, vs_scales, offs, offs2, offs3, offs4, offs5, offs6, offs7):
    idx = unstriped(offs)
    idx2 = unstriped8(offs2)
    idx3 = unstriped8(offs3)
    idx4 = unstriped8(offs4)
    idx5 = unstriped8(offs5)
    idx6 = unstriped8(offs6)
    idx7 = unstriped(offs7)
    xtu = unpack_weight(xt_words, xt_scales, "e4m3")
    wu = unpack_weight(w_words, w_scales, "e4m3")
    w2u = unpack_weight(w2_words, w2_scales, "e2m1")
    vsu = unpack_weight(vs_words, vs_scales, "e2m1")
    xtidxg = xtu[:, idx]
    a = wu.T @ xtidxg
    b = w2u.T @ xtidxg
    pw = np.zeros((R, C))
    pw[np.arange(R)[:, None], idx2[np.arange(R) % 512 // 64]] = a
    h1 = pick8(pw, idx3, 64) * f64(sa)
    pv = np.zeros((R, D))
    pv[np.arange(R)[:, None], idx4[np.arange(R) % 512 // 64]] = h1
    pu = np.zeros((R, D))
    pu[np.arange(R)[:, None], idx5[np.arange(R) % 512 // 64]] = b
    pg = pv + pu
    hid = pick8(pg, idx6, 64) * f64(sb)
    vsidx7g = vsu[:, idx7]
    hidq = mxq(hid, 0, "e4m3")
    y = vsidx7g.T @ hidq
    return y

@@ -1,0 +1,199 @@
+from contextlib import ExitStack
+
+import concourse.mybir as mybir
+
+F32 = mybir.dt.float32
+BF16 = mybir.dt.bfloat16
+I32 = mybir.dt.int32
+U32 = mybir.dt.uint32
+U16 = mybir.dt.uint16
+U8 = mybir.dt.uint8
+FP8X4 = mybir.dt.float8_e4m3fn_x4
+FP4X4 = mybir.dt.float4_e2m1fn_x4
+COPY = mybir.ActivationFunctionType.Copy
+ADD = mybir.AluOpType.add
+
+P = 128
+PACK = 4
+K, J, R, T, C, D, O, S, N, Z = 512, 256, 512, 1024, 512, 512, 256, 128, 256, 1024
+HALF = 128
+FLOPS = 2 * K * R * J * 2 + 2 * R * N * O
+
+
+def tile_picked_tokens_plain_twin_relaysum_store_plain_kernel(
+    tc, xt_words, xt_scales, w_words, w_scales, w2_words, w2_scales, sa, sb, vs_words, vs_scales,
+    offs, offs2, offs3, offs4, offs5, offs6, offs7, out,
+):
+    nc = tc.nc
+    with ExitStack() as ctx:
+        keep = ctx.enter_context(tc.tile_pool(name="keep", bufs=1))
+        psum = ctx.enter_context(tc.psum_pool(name="psum", bufs=8))
+
+        def sbuf(name, shape, dtype, tag=None):
+            return keep.tile(shape, dtype, name=name, tag=tag or name, align_bytes=64)
+
+        def load_list(name, src):
+            tile = sbuf(name, list(src.shape), U16)
+            nc.sync.dma_start(tile[:], src)
+            return tile
+
+        def load_scale_rows(queue, tile, src, q):
+            rows = src[0, 4 * q : 4 * q + 4, :].bitcast(I32)
+            queue.dma_start(tile[32 * q : 32 * q + 32, :].bitcast(I32), rows.unsqueeze(0).broadcast_to([8, 4, rows.shape[1]]))
+
+        def board(name, tag=None):
+            tile = sbuf(name, [P, D], F32, tag)
+            nc.vector.memset(tile[:], 0.0)
+            return tile
+
+        def entries(lst, lo, hi):
+            return lst[:, lo // 16 : hi // 16]
+
+        x_scale_win = sbuf("x_scale_win", [P, T], U8)
+        w2_scale_raw = sbuf("w2_scale_raw", [P, R], U8)
+        nc.vector.memset(w2_scale_raw[:].bitcast(I32), 0)
+        l_tok = load_list("l_tok", offs)
+        w2_scale_stage = sbuf("w2_scale_stage", [4, 4, R // 4], I32)
+        nc.sync.dma_start(w2_scale_stage[:], w2_scales[0].bitcast(I32).rearrange("(q b) n -> b q n", q=4))
+        for q in range(4):
+            load_scale_rows(nc.scalar if q < 3 else nc.sync, x_scale_win, xt_scales, q)
+        w2_raw = sbuf("w2_raw", [P, 2 * R], U8)
+        nc.sync.dma_start(w2_raw[:].bitcast(I32), w2_words[0].bitcast(I32))
+        x_win = sbuf("x_win", [P, T], U32)
+        nc.sync.dma_start(x_win[:].bitcast(I32), xt_words[0].rearrange("p n t -> p (n t)").bitcast(I32))
+        l_b = load_list("l_b", offs5)
+        pu = [board("pu%d" % t) for t in range(PACK)]
+
+        w_scale_raw = sbuf("w_scale_raw", [P, R], U8)
+        vs_scale_win = sbuf("vs_scale_win", [P, Z], U8)
+        for q in range(4):
+            load_scale_rows(nc.sync, w_scale_raw, w_scales, q)
+        w_raw = sbuf("w_raw", [P, R], I32)
+        nc.sync.dma_start(w_raw[:], w_words[0].rearrange("p n t -> p (n t)").bitcast(I32))
+        l_a = load_list("l_a", offs2)
+        l_relay_in = load_list("l_relay_in", offs3)
+        l_relay_out = load_list("l_relay_out", offs4)
+        sa_t = sbuf("sa_t", [P, PACK], F32)
+        nc.sync.dma_start(sa_t[:], sa.rearrange("(p t) o -> p (t o)", t=PACK))
+        l_store = load_list("l_store", offs7)
+        for q in range(4):
+            load_scale_rows(nc.sync, vs_scale_win, vs_scales, q)
+        vs_win = sbuf("vs_win", [P, Z], U16)
+        nc.sync.dma_start(vs_win[:].bitcast(I32), vs_words[0].bitcast(I32))
+        l_read = load_list("l_read", offs6)
+        sb_t = sbuf("sb_t", [P, PACK], F32)
+        nc.sync.dma_start(sb_t[:], sb.rearrange("(p t) o -> p (t o)", t=PACK))
+
+        x_words = sbuf("x_words", [P, J], U32)
+        x_scales = sbuf("x_scales", [P, J], U8)
+        w2_first = sbuf("w2_first", [P, P, 2], U8)
+        w2_first_scale = sbuf("w2_first_scale", [P, P], U8)
+        w2_view = w2_raw[:].rearrange("p (m t b) -> p t m b", t=PACK, b=2)
+        for q in range(4):
+            nc.vector.tensor_copy(w2_scale_raw[32 * q : 32 * q + 4, :].bitcast(I32), w2_scale_stage[:, q])
+        w2_scale_view = w2_scale_raw[:].rearrange("p (m t) -> p t m", t=PACK)
+        nc.vector.tensor_copy(x_scales[:, 0:HALF], x_scale_win[:].indirect(entries(l_tok, 0, HALF)))
+        nc.vector.tensor_copy(w2_first_scale[:], w2_scale_view[:, 0])
+        nc.vector.tensor_copy(w2_first[:], w2_view[:, 0])
+        nc.vector.tensor_copy(x_words[:, 0:HALF], x_win[:].indirect(entries(l_tok, 0, HALF)))
+        nc.vector.tensor_copy(x_scales[:, HALF:J], x_scale_win[:].indirect(entries(l_tok, HALF, J)))
+        nc.vector.tensor_copy(x_words[:, HALF:J], x_win[:].indirect(entries(l_tok, HALF, J)))
+
+        def first_product(dst, lhsT, lhsT_scale, lo, hi, on_scalar=False):
+            acc = psum.tile([P, hi - lo], F32, name="acc", tag="acc")
+            nc.tensor.matmul_mx(
+                out=acc[:], lhsT=lhsT, lhsT_scale=lhsT_scale,
+                rhs=x_words[:, lo:hi].bitcast(FP8X4), rhs_scale=x_scales[:, lo:hi], start=True, stop=True,
+            )
+            if on_scalar:
+                nc.scalar.activation(dst[:, lo:hi], acc[:], COPY)
+            else:
+                nc.vector.tensor_copy(dst[:, lo:hi], acc[:])
+
+        for t in range(PACK):
+            if t == 1:
+                w2_rest = sbuf("w2_rest", [P, PACK - 1, P, 2], U8, "x_win")
+                w2_rest_scale = sbuf("w2_rest_scale", [P, PACK - 1, P], U8, "w2_first_scale")
+            if t >= 1:
+                nc.vector.tensor_copy(w2_rest[:, t - 1], w2_view[:, t])
+                nc.vector.tensor_copy(w2_rest_scale[:, t - 1], w2_scale_view[:, t])
+            b_t = sbuf("b%d" % t, [P, J], F32)
+            words = w2_first[:] if t == 0 else w2_rest[:, t - 1]
+            scale = w2_first_scale[:] if t == 0 else w2_rest_scale[:, t - 1]
+            lhsT = words.rearrange("p m b -> p (m b)").bitcast(FP4X4)
+            for lo, hi in ((0, HALF), (HALF, J)) if t == 0 else ((0, J),):
+                first_product(b_t, lhsT, scale, lo, hi, t == 0 and lo == 0)
+                nc.scalar.activation(pu[t][:].indirect(entries(l_b, lo, hi)), b_t[:, lo:hi], COPY)
+
+        pw = [board("pw0", "w2_raw"), board("pw1", "w2_scale_raw")]
+        w_dealt = sbuf("w_dealt", [P, PACK, P], I32, "x_win")
+        w_scale = sbuf("w_scale", [P, PACK, P], U8, "w2_first_scale")
+        nc.vector.tensor_copy(w_scale[:], w_scale_raw[:].rearrange("p (m t) -> p t m", t=PACK))
+        nc.vector.tensor_copy(w_dealt[:], w_raw[:].rearrange("p (m t) -> p t m", t=PACK))
+        a = []
+        for t in range(PACK):
+            a_t = sbuf("a%d" % t, [P, J], F32)
+            first_product(a_t, w_dealt[:, t].bitcast(FP8X4), w_scale[:, t], 0, J)
+            a.append(a_t)
+
+        vs_sel = sbuf("vs_sel", [P, N], U16, "x_win")
+        vs_sel_scale = sbuf("vs_sel_scale", [P, N], U8, "w2_first_scale")
+        nc.vector.tensor_copy(vs_sel_scale[:], vs_scale_win[:].indirect(l_store[:]))
+        nc.vector.tensor_copy(vs_sel[:], vs_win[:].indirect(l_store[:]))
+        pv = [board("pv0", "w_raw"), board("pv1", "w_scale_raw")]
+
+        h1 = [sbuf("h1_%d" % t, [P, S], F32) for t in range(PACK)]
+        pg = [sbuf("pg%d" % t, [P, D], F32) for t in range(PACK)]
+
+        def put_a(t):
+            nc.scalar.activation(pw[t % 2][:].indirect(l_a[:]), a[t][:], COPY)
+
+        def fetch_relay(t):
+            nc.scalar.activation(h1[t][:], pw[t % 2][:].indirect(l_relay_in[:]), COPY, scale=sa_t[:, t : t + 1])
+
+        def put_relay(t):
+            nc.scalar.activation(pv[t % 2][:].indirect(l_relay_out[:]), h1[t][:], COPY)
+            nc.vector.tensor_tensor(pg[t][:], pv[t % 2][:], pu[t][:], ADD)
+
+        put_a(0)
+        put_a(1)
+        fetch_relay(0)
+        fetch_relay(1)
+        put_relay(0)
+        put_a(2)
+        put_relay(1)
+        put_a(3)
+        fetch_relay(2)
+        fetch_relay(3)
+        put_relay(2)
+        put_relay(3)
+
+        out_view = out.rearrange("(u p) o -> p u o", p=P)
+        for h in range(2):
+            lo, hi = h * HALF, (h + 1) * HALF
+            hid = sbuf("hid%d" % h, [P, PACK, HALF], BF16)
+            for t in range(PACK):
+                nc.scalar.activation(hid[:, t], pg[t][:].indirect(entries(l_read, lo, hi)), COPY, scale=sb_t[:, t : t + 1])
+            woven = sbuf("woven%d" % h, [P, HALF, PACK], BF16)
+            nc.vector.tensor_copy(
+                woven[:].rearrange("p (c i) t -> p c t i", i=4), hid[:].rearrange("p t (c i) -> p c t i", i=4)
+            )
+            hid_words = sbuf("hid_words%d" % h, [P, HALF], U32)
+            hid_scales = sbuf("hid_scales%d" % h, [P, HALF], U8)
+            nc.vector.quantize_mx(
+                out=hid_words[:].bitcast(FP8X4), scales=hid_scales[:], in_=woven[:].rearrange("p o t -> p (o t)")
+            )
+            for u in range(2):
+                acc = psum.tile([P, HALF], F32, name="acc", tag="acc")
+                nc.tensor.matmul_mx(
+                    out=acc[:], lhsT=vs_sel[:, u * P : (u + 1) * P].bitcast(FP4X4),
+                    lhsT_scale=vs_sel_scale[:, u * P : (u + 1) * P],
+                    rhs=hid_words[:].bitcast(FP8X4), rhs_scale=hid_scales[:], start=True, stop=True,
+                )
+                res = sbuf("res%d_%d" % (h, u), [P, HALF], F32)
+                if h == 1 and u == 1:
+                    nc.scalar.copy(res[:], acc[:])
+                    nc.scalar.dma_start(out_view[:, u, lo:hi], res[:])
+                else:
+                    nc.vector.tensor_copy(res[:], acc[:])
+                    nc.sync.dma_start(out_view[:, u, lo:hi], res[:])

@@ -41,9 +41,9 @@ def tile_picked_tokens_plain_twin_relaysum_store_plain_kernel(
             rows = src[0, 4 * q : 4 * q + 4, :].bitcast(I32)
             queue.dma_start(tile[32 * q : 32 * q + 32, :].bitcast(I32), rows.unsqueeze(0).broadcast_to([8, 4, rows.shape[1]]))
 
-        def board(name, tag=None):
+        def board(engine, name, tag=None):
             tile = sbuf(name, [P, D], F32, tag)
-            nc.vector.memset(tile[:], 0.0)
+            engine.memset(tile[:], 0.0)
             return tile
 
         def entries(lst, lo, hi):
@@ -52,9 +52,9 @@ def tile_picked_tokens_plain_twin_relaysum_store_plain_kernel(
         x_scale_win = sbuf("x_scale_win", [P, T], U8)
         w2_scale_raw = sbuf("w2_scale_raw", [P, R], U8)
         nc.vector.memset(w2_scale_raw[:].bitcast(I32), 0)
-        l_tok = load_list("l_tok", offs)
         w2_scale_stage = sbuf("w2_scale_stage", [4, 4, R // 4], I32)
         nc.sync.dma_start(w2_scale_stage[:], w2_scales[0].bitcast(I32).rearrange("(q b) n -> b q n", q=4))
+        l_tok = load_list("l_tok", offs)
         for q in range(4):
             load_scale_rows(nc.scalar if q < 3 else nc.sync, x_scale_win, xt_scales, q)
         w2_raw = sbuf("w2_raw", [P, 2 * R], U8)
@@ -62,7 +62,7 @@ def tile_picked_tokens_plain_twin_relaysum_store_plain_kernel(
         x_win = sbuf("x_win", [P, T], U32)
         nc.sync.dma_start(x_win[:].bitcast(I32), xt_words[0].rearrange("p n t -> p (n t)").bitcast(I32))
         l_b = load_list("l_b", offs5)
-        pu = [board("pu%d" % t) for t in range(PACK)]
+        pu = [board(nc.vector if t == 0 else nc.gpsimd, "pu%d" % t) for t in range(PACK)]
 
         w_scale_raw = sbuf("w_scale_raw", [P, R], U8)
         vs_scale_win = sbuf("vs_scale_win", [P, Z], U8)
@@ -86,74 +86,87 @@ def tile_picked_tokens_plain_twin_relaysum_store_plain_kernel(
 
         x_words = sbuf("x_words", [P, J], U32)
         x_scales = sbuf("x_scales", [P, J], U8)
-        w2_first = sbuf("w2_first", [P, P, 2], U8)
-        w2_first_scale = sbuf("w2_first_scale", [P, P], U8)
+        w2_first = sbuf("w2_first", [P, 2, P, 2], U8)
+        w2_first_scale = sbuf("w2_first_scale", [P, 2, P], U8)
         w2_view = w2_raw[:].rearrange("p (m t b) -> p t m b", t=PACK, b=2)
         for q in range(4):
             nc.vector.tensor_copy(w2_scale_raw[32 * q : 32 * q + 4, :].bitcast(I32), w2_scale_stage[:, q])
         w2_scale_view = w2_scale_raw[:].rearrange("p (m t) -> p t m", t=PACK)
         nc.vector.tensor_copy(x_scales[:, 0:HALF], x_scale_win[:].indirect(entries(l_tok, 0, HALF)))
-        nc.vector.tensor_copy(w2_first_scale[:], w2_scale_view[:, 0])
-        nc.vector.tensor_copy(w2_first[:], w2_view[:, 0])
+        nc.vector.tensor_copy(w2_first_scale[:], w2_scale_view[:, 0:2])
+        nc.vector.tensor_copy(w2_first[:], w2_view[:, 0:2])
         nc.vector.tensor_copy(x_words[:, 0:HALF], x_win[:].indirect(entries(l_tok, 0, HALF)))
         nc.vector.tensor_copy(x_scales[:, HALF:J], x_scale_win[:].indirect(entries(l_tok, HALF, J)))
         nc.vector.tensor_copy(x_words[:, HALF:J], x_win[:].indirect(entries(l_tok, HALF, J)))
 
-        def first_product(dst, lhsT, lhsT_scale, lo, hi, on_scalar=False):
-            acc = psum.tile([P, hi - lo], F32, name="acc", tag="acc")
+        def product(acc, words, scale, dtype, lo, hi):
             nc.tensor.matmul_mx(
-                out=acc[:], lhsT=lhsT, lhsT_scale=lhsT_scale,
+                out=acc, lhsT=words.bitcast(dtype), lhsT_scale=scale,
                 rhs=x_words[:, lo:hi].bitcast(FP8X4), rhs_scale=x_scales[:, lo:hi], start=True, stop=True,
             )
-            if on_scalar:
-                nc.scalar.activation(dst[:, lo:hi], acc[:], COPY)
+
+        def put_b(t, src, lo, hi):
+            nc.scalar.activation(pu[t][:].indirect(entries(l_b, lo, hi)), src, COPY)
+
+        for t in range(2):
+            acc = psum.tile([P, HALF], F32, name="acc", tag="acc")
+            product(acc[:], w2_first[:, t].rearrange("p m b -> p (m b)"), w2_first_scale[:, t], FP4X4, 0, HALF)
+            b_lo = sbuf("b_lo%d" % t, [P, HALF], F32)
+            if t == 0:
+                nc.scalar.activation(b_lo[:], acc[:], COPY)
             else:
-                nc.vector.tensor_copy(dst[:, lo:hi], acc[:])
-
-        for t in range(PACK):
-            if t == 1:
-                w2_rest = sbuf("w2_rest", [P, PACK - 1, P, 2], U8, "x_win")
-                w2_rest_scale = sbuf("w2_rest_scale", [P, PACK - 1, P], U8, "w2_first_scale")
-            if t >= 1:
-                nc.vector.tensor_copy(w2_rest[:, t - 1], w2_view[:, t])
-                nc.vector.tensor_copy(w2_rest_scale[:, t - 1], w2_scale_view[:, t])
+                nc.vector.tensor_copy(b_lo[:], acc[:])
+            put_b(t, b_lo[:], 0, HALF)
+        acc = psum.tile([P, 2, HALF], F32, name="acc", tag="acc")
+        for t in range(2):
+            product(acc[:, t], w2_first[:, t].rearrange("p m b -> p (m b)"), w2_first_scale[:, t], FP4X4, HALF, J)
+        b_hi = sbuf("b_hi", [P, 2, HALF], F32)
+        nc.vector.tensor_copy(b_hi[:], acc[:])
+        for t in range(2):
+            put_b(t, b_hi[:, t], HALF, J)
+        w2_rest = sbuf("w2_rest", [P, 2, P, 2], U8, "x_win")
+        w2_rest_scale = sbuf("w2_rest_scale", [P, 2, P], U8, "w2_first_scale")
+        nc.vector.tensor_copy(w2_rest[:], w2_view[:, 2:PACK])
+        nc.vector.tensor_copy(w2_rest_scale[:], w2_scale_view[:, 2:PACK])
+        for t in range(2, PACK):
+            acc = psum.tile([P, J], F32, name="acc", tag="acc")
+            product(acc[:], w2_rest[:, t - 2].rearrange("p m b -> p (m b)"), w2_rest_scale[:, t - 2], FP4X4, 0, J)
             b_t = sbuf("b%d" % t, [P, J], F32)
-            words = w2_first[:] if t == 0 else w2_rest[:, t - 1]
-            scale = w2_first_scale[:] if t == 0 else w2_rest_scale[:, t - 1]
-            lhsT = words.rearrange("p m b -> p (m b)").bitcast(FP4X4)
-            for lo, hi in ((0, HALF), (HALF, J)) if t == 0 else ((0, J),):
-                first_product(b_t, lhsT, scale, lo, hi, t == 0 and lo == 0)
-                nc.scalar.activation(pu[t][:].indirect(entries(l_b, lo, hi)), b_t[:, lo:hi], COPY)
+            nc.vector.tensor_copy(b_t[:], acc[:])
+            put_b(t, b_t[:], 0, J)
 
-        pw = [board("pw0", "w2_raw"), board("pw1", "w2_scale_raw")]
         w_dealt = sbuf("w_dealt", [P, PACK, P], I32, "x_win")
         w_scale = sbuf("w_scale", [P, PACK, P], U8, "w2_first_scale")
         nc.vector.tensor_copy(w_scale[:], w_scale_raw[:].rearrange("p (m t) -> p t m", t=PACK))
         nc.vector.tensor_copy(w_dealt[:], w_raw[:].rearrange("p (m t) -> p t m", t=PACK))
+        pw = [board(nc.gpsimd, "pw%d" % t, "b_lo%d" % t) for t in range(2)]
         a = []
-        for t in range(PACK):
-            a_t = sbuf("a%d" % t, [P, J], F32)
-            first_product(a_t, w_dealt[:, t].bitcast(FP8X4), w_scale[:, t], 0, J)
-            a.append(a_t)
+        for pair in range(2):
+            acc = psum.tile([P, 2, J], F32, name="acc", tag="acc")
+            for i in range(2):
+                t = 2 * pair + i
+                product(acc[:, i], w_dealt[:, t], w_scale[:, t], FP8X4, 0, J)
+            a.append(sbuf("a%d" % pair, [P, 2, J], F32))
+            nc.vector.tensor_copy(a[pair][:], acc[:])
 
         vs_sel = sbuf("vs_sel", [P, N], U16, "x_win")
         vs_sel_scale = sbuf("vs_sel_scale", [P, N], U8, "w2_first_scale")
         nc.vector.tensor_copy(vs_sel_scale[:], vs_scale_win[:].indirect(l_store[:]))
         nc.vector.tensor_copy(vs_sel[:], vs_win[:].indirect(l_store[:]))
-        pv = [board("pv0", "w_raw"), board("pv1", "w_scale_raw")]
+        pv = [board(nc.gpsimd, "pv%d" % t, tag) for t, tag in enumerate(("b_hi", "b2", "w_raw", "w_scale_raw"))]
 
         h1 = [sbuf("h1_%d" % t, [P, S], F32) for t in range(PACK)]
         pg = [sbuf("pg%d" % t, [P, D], F32) for t in range(PACK)]
 
         def put_a(t):
-            nc.scalar.activation(pw[t % 2][:].indirect(l_a[:]), a[t][:], COPY)
+            nc.scalar.activation(pw[t % 2][:].indirect(l_a[:]), a[t // 2][:, t % 2], COPY)
 
         def fetch_relay(t):
             nc.scalar.activation(h1[t][:], pw[t % 2][:].indirect(l_relay_in[:]), COPY, scale=sa_t[:, t : t + 1])
 
         def put_relay(t):
-            nc.scalar.activation(pv[t % 2][:].indirect(l_relay_out[:]), h1[t][:], COPY)
-            nc.vector.tensor_tensor(pg[t][:], pv[t % 2][:], pu[t][:], ADD)
+            nc.scalar.activation(pv[t][:].indirect(l_relay_out[:]), h1[t][:], COPY)
+            nc.vector.tensor_tensor(pg[t][:], pv[t][:], pu[t][:], ADD)
 
         put_a(0)
         put_a(1)
@@ -169,19 +182,27 @@ def tile_picked_tokens_plain_twin_relaysum_store_plain_kernel(
         put_relay(3)
 
         out_view = out.rearrange("(u p) o -> p u o", p=P)
+        hid = sbuf("hid", [P, PACK, O], BF16, "h1_2")
+
+        def fetch_hid(t, lo, hi):
+            nc.scalar.activation(hid[:, t, lo:hi], pg[t][:].indirect(entries(l_read, lo, hi)), COPY, scale=sb_t[:, t : t + 1])
+
+        for t in range(PACK - 1):
+            fetch_hid(t, 0, O)
+        woven = []
         for h in range(2):
             lo, hi = h * HALF, (h + 1) * HALF
-            hid = sbuf("hid%d" % h, [P, PACK, HALF], BF16)
-            for t in range(PACK):
-                nc.scalar.activation(hid[:, t], pg[t][:].indirect(entries(l_read, lo, hi)), COPY, scale=sb_t[:, t : t + 1])
-            woven = sbuf("woven%d" % h, [P, HALF, PACK], BF16)
+            fetch_hid(PACK - 1, lo, hi)
+            woven.append(sbuf("woven%d" % h, [P, HALF, PACK], BF16))
             nc.vector.tensor_copy(
-                woven[:].rearrange("p (c i) t -> p c t i", i=4), hid[:].rearrange("p t (c i) -> p c t i", i=4)
+                woven[h][:].rearrange("p (c i) t -> p c t i", i=4), hid[:, :, lo:hi].rearrange("p t (c i) -> p c t i", i=4)
             )
+        for h in range(2):
+            lo, hi = h * HALF, (h + 1) * HALF
             hid_words = sbuf("hid_words%d" % h, [P, HALF], U32)
             hid_scales = sbuf("hid_scales%d" % h, [P, HALF], U8)
             nc.vector.quantize_mx(
-                out=hid_words[:].bitcast(FP8X4), scales=hid_scales[:], in_=woven[:].rearrange("p o t -> p (o t)")
+                out=hid_words[:].bitcast(FP8X4), scales=hid_scales[:], in_=woven[h][:].rearrange("p o t -> p (o t)")
             )
             for u in range(2):
                 acc = psum.tile([P, HALF], F32, name="acc", tag="acc")

@@ -54,11 +54,11 @@ def tile_picked_tokens_plain_twin_relaysum_store_plain_kernel(
         nc.vector.memset(w2_scale_raw[:].bitcast(I32), 0)
         w2_scale_stage = sbuf("w2_scale_stage", [4, 4, R // 4], I32)
         nc.sync.dma_start(w2_scale_stage[:], w2_scales[0].bitcast(I32).rearrange("(q b) n -> b q n", q=4))
+        w2_raw = sbuf("w2_raw", [P, 2 * R], U8)
+        nc.sync.dma_start(w2_raw[:].bitcast(I32), w2_words[0].bitcast(I32))
         l_tok = load_list("l_tok", offs)
         for q in range(4):
             load_scale_rows(nc.scalar if q < 3 else nc.sync, x_scale_win, xt_scales, q)
-        w2_raw = sbuf("w2_raw", [P, 2 * R], U8)
-        nc.sync.dma_start(w2_raw[:].bitcast(I32), w2_words[0].bitcast(I32))
         x_win = sbuf("x_win", [P, T], U32)
         nc.sync.dma_start(x_win[:].bitcast(I32), xt_words[0].rearrange("p n t -> p (n t)").bitcast(I32))
         l_b = load_list("l_b", offs5)
@@ -86,7 +86,7 @@ def tile_picked_tokens_plain_twin_relaysum_store_plain_kernel(
 
         x_words = sbuf("x_words", [P, J], U32)
         x_scales = sbuf("x_scales", [P, J], U8)
-        w2_first = sbuf("w2_first", [P, 2, P, 2], U8)
+        w2_first = sbuf("w2_first", [P, 2, P], U16)
         w2_first_scale = sbuf("w2_first_scale", [P, 2, P], U8)
         w2_view = w2_raw[:].rearrange("p (m t b) -> p t m b", t=PACK, b=2)
         for q in range(4):
@@ -94,7 +94,7 @@ def tile_picked_tokens_plain_twin_relaysum_store_plain_kernel(
         w2_scale_view = w2_scale_raw[:].rearrange("p (m t) -> p t m", t=PACK)
         nc.vector.tensor_copy(x_scales[:, 0:HALF], x_scale_win[:].indirect(entries(l_tok, 0, HALF)))
         nc.vector.tensor_copy(w2_first_scale[:], w2_scale_view[:, 0:2])
-        nc.vector.tensor_copy(w2_first[:], w2_view[:, 0:2])
+        nc.scalar.copy(w2_first[:], w2_raw[:].bitcast(U16).rearrange("p (m t) -> p t m", t=PACK)[:, 0:2])
         nc.vector.tensor_copy(x_words[:, 0:HALF], x_win[:].indirect(entries(l_tok, 0, HALF)))
         nc.vector.tensor_copy(x_scales[:, HALF:J], x_scale_win[:].indirect(entries(l_tok, HALF, J)))
         nc.vector.tensor_copy(x_words[:, HALF:J], x_win[:].indirect(entries(l_tok, HALF, J)))
@@ -110,7 +110,7 @@ def tile_picked_tokens_plain_twin_relaysum_store_plain_kernel(
 
         for t in range(2):
             acc = psum.tile([P, HALF], F32, name="acc", tag="acc")
-            product(acc[:], w2_first[:, t].rearrange("p m b -> p (m b)"), w2_first_scale[:, t], FP4X4, 0, HALF)
+            product(acc[:], w2_first[:, t], w2_first_scale[:, t], FP4X4, 0, HALF)
             b_lo = sbuf("b_lo%d" % t, [P, HALF], F32)
             if t == 0:
                 nc.scalar.activation(b_lo[:], acc[:], COPY)
@@ -119,7 +119,7 @@ def tile_picked_tokens_plain_twin_relaysum_store_plain_kernel(
             put_b(t, b_lo[:], 0, HALF)
         acc = psum.tile([P, 2, HALF], F32, name="acc", tag="acc")
         for t in range(2):
-            product(acc[:, t], w2_first[:, t].rearrange("p m b -> p (m b)"), w2_first_scale[:, t], FP4X4, HALF, J)
+            product(acc[:, t], w2_first[:, t], w2_first_scale[:, t], FP4X4, HALF, J)
         b_hi = sbuf("b_hi", [P, 2, HALF], F32)
         nc.vector.tensor_copy(b_hi[:], acc[:])
         for t in range(2):

from contextlib import ExitStack

import concourse.mybir as mybir

F32 = mybir.dt.float32
BF16 = mybir.dt.bfloat16
I32 = mybir.dt.int32
U32 = mybir.dt.uint32
U16 = mybir.dt.uint16
U8 = mybir.dt.uint8
FP8X4 = mybir.dt.float8_e4m3fn_x4
FP4X4 = mybir.dt.float4_e2m1fn_x4
COPY = mybir.ActivationFunctionType.Copy
ADD = mybir.AluOpType.add

P = 128
PACK = 4
K, J, R, T, C, D, O, S, N, Z = 512, 256, 512, 1024, 512, 512, 256, 128, 256, 1024
HALF = 128
FLOPS = 2 * K * R * J * 2 + 2 * R * N * O


def tile_picked_tokens_plain_twin_relaysum_store_plain_kernel(
    tc, xt_words, xt_scales, w_words, w_scales, w2_words, w2_scales, sa, sb, vs_words, vs_scales,
    offs, offs2, offs3, offs4, offs5, offs6, offs7, out,
):
    nc = tc.nc
    with ExitStack() as ctx:
        keep = ctx.enter_context(tc.tile_pool(name="keep", bufs=1))
        psum = ctx.enter_context(tc.psum_pool(name="psum", bufs=8))

        def sbuf(name, shape, dtype, tag=None):
            return keep.tile(shape, dtype, name=name, tag=tag or name, align_bytes=64)

        def load_list(name, src):
            tile = sbuf(name, list(src.shape), U16)
            nc.sync.dma_start(tile[:], src)
            return tile

        def load_scale_rows(queue, tile, src, q):
            rows = src[0, 4 * q : 4 * q + 4, :].bitcast(I32)
            queue.dma_start(tile[32 * q : 32 * q + 32, :].bitcast(I32), rows.unsqueeze(0).broadcast_to([8, 4, rows.shape[1]]))

        def board(engine, name, tag=None):
            tile = sbuf(name, [P, D], F32, tag)
            engine.memset(tile[:], 0.0)
            return tile

        def entries(lst, lo, hi):
            return lst[:, lo // 16 : hi // 16]

        x_scale_win = sbuf("x_scale_win", [P, T], U8)
        w2_scale_raw = sbuf("w2_scale_raw", [P, R], U8)
        nc.vector.memset(w2_scale_raw[:].bitcast(I32), 0)
        w2_scale_stage = sbuf("w2_scale_stage", [4, 4, R // 4], I32)
        nc.sync.dma_start(w2_scale_stage[:], w2_scales[0].bitcast(I32).rearrange("(q b) n -> b q n", q=4))
        w2_raw = sbuf("w2_raw", [P, 2 * R], U8)
        nc.sync.dma_start(w2_raw[:].bitcast(I32), w2_words[0].bitcast(I32))
        l_tok = load_list("l_tok", offs)
        for q in range(4):
            load_scale_rows(nc.scalar if q < 3 else nc.sync, x_scale_win, xt_scales, q)
        x_win = sbuf("x_win", [P, T], U32)
        nc.sync.dma_start(x_win[:].bitcast(I32), xt_words[0].rearrange("p n t -> p (n t)").bitcast(I32))
        l_b = load_list("l_b", offs5)
        pu = [board(nc.vector if t == 0 else nc.gpsimd, "pu%d" % t) for t in range(PACK)]

        w_scale_raw = sbuf("w_scale_raw", [P, R], U8)
        vs_scale_win = sbuf("vs_scale_win", [P, Z], U8)
        for q in range(4):
            load_scale_rows(nc.sync, w_scale_raw, w_scales, q)
        w_raw = sbuf("w_raw", [P, R], I32)
        nc.sync.dma_start(w_raw[:], w_words[0].rearrange("p n t -> p (n t)").bitcast(I32))
        l_a = load_list("l_a", offs2)
        l_relay_in = load_list("l_relay_in", offs3)
        l_relay_out = load_list("l_relay_out", offs4)
        sa_t = sbuf("sa_t", [P, PACK], F32)
        nc.sync.dma_start(sa_t[:], sa.rearrange("(p t) o -> p (t o)", t=PACK))
        l_store = load_list("l_store", offs7)
        for q in range(4):
            load_scale_rows(nc.sync, vs_scale_win, vs_scales, q)
        vs_win = sbuf("vs_win", [P, Z], U16)
        nc.sync.dma_start(vs_win[:].bitcast(I32), vs_words[0].bitcast(I32))
        l_read = load_list("l_read", offs6)
        sb_t = sbuf("sb_t", [P, PACK], F32)
        nc.sync.dma_start(sb_t[:], sb.rearrange("(p t) o -> p (t o)", t=PACK))

        x_words = sbuf("x_words", [P, J], U32)
        x_scales = sbuf("x_scales", [P, J], U8)
        w2_first = sbuf("w2_first", [P, 2, P], U16)
        w2_first_scale = sbuf("w2_first_scale", [P, 2, P], U8)
        w2_view = w2_raw[:].rearrange("p (m t b) -> p t m b", t=PACK, b=2)
        for q in range(4):
            nc.vector.tensor_copy(w2_scale_raw[32 * q : 32 * q + 4, :].bitcast(I32), w2_scale_stage[:, q])
        w2_scale_view = w2_scale_raw[:].rearrange("p (m t) -> p t m", t=PACK)
        nc.vector.tensor_copy(x_scales[:, 0:HALF], x_scale_win[:].indirect(entries(l_tok, 0, HALF)))
        nc.vector.tensor_copy(w2_first_scale[:], w2_scale_view[:, 0:2])
        nc.scalar.copy(w2_first[:], w2_raw[:].bitcast(U16).rearrange("p (m t) -> p t m", t=PACK)[:, 0:2])
        nc.vector.tensor_copy(x_words[:, 0:HALF], x_win[:].indirect(entries(l_tok, 0, HALF)))
        nc.vector.tensor_copy(x_scales[:, HALF:J], x_scale_win[:].indirect(entries(l_tok, HALF, J)))
        nc.vector.tensor_copy(x_words[:, HALF:J], x_win[:].indirect(entries(l_tok, HALF, J)))

        def product(acc, words, scale, dtype, lo, hi):
            nc.tensor.matmul_mx(
                out=acc, lhsT=words.bitcast(dtype), lhsT_scale=scale,
                rhs=x_words[:, lo:hi].bitcast(FP8X4), rhs_scale=x_scales[:, lo:hi], start=True, stop=True,
            )

        def put_b(t, src, lo, hi):
            nc.scalar.activation(pu[t][:].indirect(entries(l_b, lo, hi)), src, COPY)

        for t in range(2):
            acc = psum.tile([P, HALF], F32, name="acc", tag="acc")
            product(acc[:], w2_first[:, t], w2_first_scale[:, t], FP4X4, 0, HALF)
            b_lo = sbuf("b_lo%d" % t, [P, HALF], F32)
            if t == 0:
                nc.scalar.activation(b_lo[:], acc[:], COPY)
            else:
                nc.vector.tensor_copy(b_lo[:], acc[:])
            put_b(t, b_lo[:], 0, HALF)
        acc = psum.tile([P, 2, HALF], F32, name="acc", tag="acc")
        for t in range(2):
            product(acc[:, t], w2_first[:, t], w2_first_scale[:, t], FP4X4, HALF, J)
        b_hi = sbuf("b_hi", [P, 2, HALF], F32)
        nc.vector.tensor_copy(b_hi[:], acc[:])
        for t in range(2):
            put_b(t, b_hi[:, t], HALF, J)
        w2_rest = sbuf("w2_rest", [P, 2, P, 2], U8, "x_win")
        w2_rest_scale = sbuf("w2_rest_scale", [P, 2, P], U8, "w2_first_scale")
        nc.vector.tensor_copy(w2_rest[:], w2_view[:, 2:PACK])
        nc.vector.tensor_copy(w2_rest_scale[:], w2_scale_view[:, 2:PACK])
        for t in range(2, PACK):
            acc = psum.tile([P, J], F32, name="acc", tag="acc")
            product(acc[:], w2_rest[:, t - 2].rearrange("p m b -> p (m b)"), w2_rest_scale[:, t - 2], FP4X4, 0, J)
            b_t = sbuf("b%d" % t, [P, J], F32)
            nc.vector.tensor_copy(b_t[:], acc[:])
            put_b(t, b_t[:], 0, J)

        w_dealt = sbuf("w_dealt", [P, PACK, P], I32, "x_win")
        w_scale = sbuf("w_scale", [P, PACK, P], U8, "w2_first_scale")
        nc.vector.tensor_copy(w_scale[:], w_scale_raw[:].rearrange("p (m t) -> p t m", t=PACK))
        nc.vector.tensor_copy(w_dealt[:], w_raw[:].rearrange("p (m t) -> p t m", t=PACK))
        pw = [board(nc.gpsimd, "pw%d" % t, "b_lo%d" % t) for t in range(2)]
        a = []
        for pair in range(2):
            acc = psum.tile([P, 2, J], F32, name="acc", tag="acc")
            for i in range(2):
                t = 2 * pair + i
                product(acc[:, i], w_dealt[:, t], w_scale[:, t], FP8X4, 0, J)
            a.append(sbuf("a%d" % pair, [P, 2, J], F32))
            nc.vector.tensor_copy(a[pair][:], acc[:])

        vs_sel = sbuf("vs_sel", [P, N], U16, "x_win")
        vs_sel_scale = sbuf("vs_sel_scale", [P, N], U8, "w2_first_scale")
        nc.vector.tensor_copy(vs_sel_scale[:], vs_scale_win[:].indirect(l_store[:]))
        nc.vector.tensor_copy(vs_sel[:], vs_win[:].indirect(l_store[:]))
        pv = [board(nc.gpsimd, "pv%d" % t, tag) for t, tag in enumerate(("b_hi", "b2", "w_raw", "w_scale_raw"))]

        h1 = [sbuf("h1_%d" % t, [P, S], F32) for t in range(PACK)]
        pg = [sbuf("pg%d" % t, [P, D], F32) for t in range(PACK)]

        def put_a(t):
            nc.scalar.activation(pw[t % 2][:].indirect(l_a[:]), a[t // 2][:, t % 2], COPY)

        def fetch_relay(t):
            nc.scalar.activation(h1[t][:], pw[t % 2][:].indirect(l_relay_in[:]), COPY, scale=sa_t[:, t : t + 1])

        def put_relay(t):
            nc.scalar.activation(pv[t][:].indirect(l_relay_out[:]), h1[t][:], COPY)
            nc.vector.tensor_tensor(pg[t][:], pv[t][:], pu[t][:], ADD)

        put_a(0)
        put_a(1)
        fetch_relay(0)
        fetch_relay(1)
        put_relay(0)
        put_a(2)
        put_relay(1)
        put_a(3)
        fetch_relay(2)
        fetch_relay(3)
        put_relay(2)
        put_relay(3)

        out_view = out.rearrange("(u p) o -> p u o", p=P)
        hid = sbuf("hid", [P, PACK, O], BF16, "h1_2")

        def fetch_hid(t, lo, hi):
            nc.scalar.activation(hid[:, t, lo:hi], pg[t][:].indirect(entries(l_read, lo, hi)), COPY, scale=sb_t[:, t : t + 1])

        for t in range(PACK - 1):
            fetch_hid(t, 0, O)
        woven = []
        for h in range(2):
            lo, hi = h * HALF, (h + 1) * HALF
            fetch_hid(PACK - 1, lo, hi)
            woven.append(sbuf("woven%d" % h, [P, HALF, PACK], BF16))
            nc.vector.tensor_copy(
                woven[h][:].rearrange("p (c i) t -> p c t i", i=4), hid[:, :, lo:hi].rearrange("p t (c i) -> p c t i", i=4)
            )
        for h in range(2):
            lo, hi = h * HALF, (h + 1) * HALF
            hid_words = sbuf("hid_words%d" % h, [P, HALF], U32)
            hid_scales = sbuf("hid_scales%d" % h, [P, HALF], U8)
            nc.vector.quantize_mx(
                out=hid_words[:].bitcast(FP8X4), scales=hid_scales[:], in_=woven[h][:].rearrange("p o t -> p (o t)")
            )
            for u in range(2):
                acc = psum.tile([P, HALF], F32, name="acc", tag="acc")
                nc.tensor.matmul_mx(
                    out=acc[:], lhsT=vs_sel[:, u * P : (u + 1) * P].bitcast(FP4X4),
                    lhsT_scale=vs_sel_scale[:, u * P : (u + 1) * P],
                    rhs=hid_words[:].bitcast(FP8X4), rhs_scale=hid_scales[:], start=True, stop=True,
                )
                res = sbuf("res%d_%d" % (h, u), [P, HALF], F32)
                if h == 1 and u == 1:
                    nc.scalar.copy(res[:], acc[:])
                    nc.scalar.dma_start(out_view[:, u, lo:hi], res[:])
                else:
                    nc.vector.tensor_copy(res[:], acc[:])
                    nc.sync.dma_start(out_view[:, u, lo:hi], res[:])
